import numpy as np
import ml_dtypes


def mxq(x, axis, fmt="e4m3"):
    dtype, down = {"e4m3": (ml_dtypes.float8_e4m3fn, 7), "e5m2": (ml_dtypes.float8_e5m2, 14)}[fmt]
    v = np.moveaxis(np.asarray(x, np.float32).astype(ml_dtypes.bfloat16).astype(np.float64), axis, -1)
    blocks = v.reshape(v.shape[:-1] + (-1, 32))
    amax = np.abs(blocks).max(-1, keepdims=True)
    byte = np.maximum(np.where(amax > 0, np.frexp(amax)[1] - 1 + 127, 0) - down, 1)
    scale = np.exp2(byte - 127.0)
    codes = (blocks / scale).astype(np.float32).astype(dtype).astype(np.float64)
    return np.moveaxis((codes * scale).reshape(v.shape), -1, axis)


WIDE = False


def mx_kscale(k, group=512):
    if not WIDE:
        return np.ones(k)
    levels = np.array([10, -10, 5, -5, 0])
    if group != 512:
        return np.exp2(np.random.permutation(np.resize(levels, k // group))).repeat(group)
    if k % 512:
        return np.exp2(np.random.permutation(np.resize(levels, k // 32))).repeat(32)
    a = np.empty((k // 512, 16))
    for p in range(k // 512):
        a[p, :8] = np.random.permutation(np.resize(levels, 8))
        for g in range(8):
            far = levels[np.abs(levels - a[p, g]) >= 10]
            a[p, g + 8] = far[np.random.randint(len(far))]
    return np.exp2(a.ravel()).repeat(32)


def f64(x):
    return np.asarray(x).astype(np.float64)


G, D, M, N = 2, 256, 256, 512


def setup_inputs():
    n = np.random.standard_normal
    s = mx_kscale(D, 0)[:, None]
    return {
        "x": (n((G, D, N)) * s).astype(np.float32),
        "w": (n((G, D, M)) / np.sqrt(D) / s).astype(np.float32),
        "u": (n((G, D, M)) / np.sqrt(D) / s).astype(np.float32),
        "b": (0.5 * n((G, M, 1))).astype(np.float32),
        "r": n((G, M, N)).astype(np.float32),
    }


def reference(x, w, u, b, r):
    xq = mxq(f64(x), 1, "e4m3")
    h = mxq(f64(w), 1, "e4m3").transpose(0, 2, 1) @ xq
    g = mxq(f64(u), 1, "e4m3").transpose(0, 2, 1) @ xq
    h = h + f64(b)
    y = np.maximum(h, 0.0) * g
    y = y + f64(r)
    return y

@@ -1,0 +1,164 @@
+from contextlib import ExitStack
+
+import concourse.mybir as mybir
+
+G, D, M, N = 2, 256, 256, 512
+FLOPS = 2 * 2 * G * D * M * N
+
+F32 = mybir.dt.float32
+BF16 = mybir.dt.bfloat16
+U32 = mybir.dt.uint32
+U8 = mybir.dt.uint8
+FP8X4 = mybir.dt.float8_e4m3fn_x4
+ALU = mybir.AluOpType
+ACT = mybir.ActivationFunctionType
+
+P = 128
+PACK = 4
+ROWS = D // PACK
+M_TILE = 128
+M_TILES = M // M_TILE
+HALF = N // 2
+RUN = 4
+SQUARE = 32
+X_SPLIT = 304
+
+
+def interleave(copy, dst, src):
+    copy(
+        out=dst.rearrange("p (c i) j -> p c j i", i=RUN),
+        in_=src.rearrange("p j (c i) -> p c j i", i=RUN),
+    )
+
+
+def quantize(nc, codes, scales, grouped):
+    nc.vector.quantize_mx(
+        out=codes.bitcast(FP8X4),
+        scales=scales,
+        in_=grouped.rearrange("p c j -> p (c j)"),
+    )
+
+
+def tile_rows_gglu_relu_bias_res_kernel(tc, x, w, u, b, r, out):
+    nc = tc.nc
+    with ExitStack() as ctx:
+        sb = ctx.enter_context(tc.tile_pool(name="sb", bufs=1))
+        psum = ctx.enter_context(tc.psum_pool(name="psum", bufs=1))
+        ctx.enter_context(tc.manual_schedule())
+
+        def features(t):
+            return t.rearrange("g (p j) c -> (g p) j c", j=PACK)
+
+        x_raw = sb.tile([P, PACK, N], F32, name="x_raw")
+        w_raw = sb.tile([P, PACK, M], F32, name="w_raw")
+        u_raw = sb.tile([P, PACK, M], F32, name="u_raw")
+        nc.sync.dma_start(out=x_raw[:], in_=features(x))
+        nc.sync.dma_start(out=w_raw[:], in_=features(w))
+        nc.sync.dma_start(out=u_raw[:], in_=features(u))
+        res = []
+        for t in range(M_TILES):
+            res_t = sb.tile([P, G, N], F32, name="res%d" % t)
+            nc.sync.dma_start(
+                out=res_t[:],
+                in_=r[:, t * M_TILE : (t + 1) * M_TILE, :].rearrange("g p n -> p g n"),
+            )
+            res.append(res_t)
+
+        b_rows = sb.tile([P, P], F32, name="b_rows", align_bytes=64)
+        b_cols = sb.tile([P, P], F32, name="b_cols", align_bytes=64)
+        nc.vector.memset(b_rows[:], 0.0)
+        nc.scalar.dma_start(
+            out=b_rows[0:P:SQUARE, :].rearrange("q (c i) -> q c i", i=SQUARE),
+            in_=b.rearrange("g (t q i) o -> q (g t) (i o)", t=M_TILES, i=SQUARE),
+        )
+        nc.vector.transpose(out=b_cols[:], in_=b_rows[:])
+
+        x_lo = sb.tile([P, HALF, PACK], BF16, name="x_lo", align_bytes=64)
+        x_hi = sb.tile([P, HALF, PACK], BF16, name="x_hi", align_bytes=64)
+        x_codes = sb.tile([P, N], U32, name="x_codes", align_bytes=64)
+        x_scales = sb.tile([P, N], U8, name="x_scales", align_bytes=64)
+
+        def weight_tiles(name):
+            tiles = []
+            for t in range(M_TILES):
+                grouped = sb.tile([P, M_TILE, PACK], BF16, name="%s_bf%d" % (name, t), align_bytes=64)
+                codes = sb.tile([P, M_TILE], U32, name="%s_codes%d" % (name, t), align_bytes=64)
+                scales = sb.tile([P, M_TILE], U8, name="%s_scales%d" % (name, t), align_bytes=64)
+                tiles.append((grouped, codes, scales))
+            return tiles
+
+        w_tiles = weight_tiles("w")
+        u_tiles = weight_tiles("u")
+
+        def m_cols(t):
+            return slice(t * M_TILE, (t + 1) * M_TILE)
+
+        def quantize_weights(tiles):
+            grouped, codes, scales = tiles
+            quantize(nc, codes[:], scales[:], grouped[:])
+
+        interleave(nc.vector.tensor_copy, x_lo[:], x_raw[:, :, 0:HALF])
+        interleave(nc.vector.tensor_copy, x_hi[:, 0 : X_SPLIT - HALF, :], x_raw[:, :, HALF:X_SPLIT])
+        interleave(nc.scalar.copy, x_hi[:, X_SPLIT - HALF : HALF, :], x_raw[:, :, X_SPLIT:N])
+        quantize(nc, x_codes[:, 0:HALF], x_scales[:, 0:HALF], x_lo[:])
+        quantize(nc, x_codes[:, HALF:N], x_scales[:, HALF:N], x_hi[:])
+
+        interleave(nc.scalar.copy, w_tiles[0][0][:], w_raw[:, :, m_cols(0)])
+        interleave(nc.vector.tensor_copy, w_tiles[1][0][:], w_raw[:, :, m_cols(1)])
+        quantize_weights(w_tiles[0])
+        interleave(nc.vector.tensor_copy, u_tiles[0][0][:], u_raw[:, :, m_cols(0)])
+        interleave(nc.scalar.copy, u_tiles[1][0][:], u_raw[:, :, m_cols(1)])
+        quantize_weights(w_tiles[1])
+        quantize_weights(u_tiles[0])
+        quantize_weights(u_tiles[1])
+
+        def product(name, tiles, g):
+            grouped, codes, scales = tiles
+            rows = slice(g * ROWS, (g + 1) * ROWS)
+            acc = psum.tile([M_TILE, N], F32, name=name)
+            nc.tensor.matmul_mx(
+                out=acc[:],
+                lhsT=codes[rows, :].bitcast(FP8X4),
+                lhsT_scale=scales[rows, :],
+                rhs=x_codes[rows, :].bitcast(FP8X4),
+                rhs_scale=x_scales[rows, :],
+                start=True,
+                stop=True,
+            )
+            return acc
+
+        order = [(t, g) for t in range(M_TILES) for g in range(G)]
+        h = {}
+        gate = {}
+        for t in range(M_TILES):
+            for g in range(G):
+                h[t, g] = product("h%d%d" % (t, g), w_tiles[t], g)
+            for g in range(G):
+                gate[t, g] = product("gate%d%d" % (t, g), u_tiles[t], g)
+
+        act = {}
+        for t, g in order:
+            col = SQUARE * (g * M_TILES + t)
+            act_tg = sb.tile([P, N], F32, name="act%d%d" % (t, g))
+            nc.scalar.activation(
+                out=act_tg[:], in_=h[t, g][:], func=ACT.Relu, bias=b_cols[:, col : col + 1]
+            )
+            act[t, g] = act_tg
+
+        gated = {}
+
+        def multiply(t, g):
+            gated_tg = sb.tile([P, N], F32, name="gated%d%d" % (t, g))
+            nc.vector.tensor_tensor(out=gated_tg[:], in0=gate[t, g][:], in1=act[t, g][:], op=ALU.mult)
+            gated[t, g] = gated_tg
+
+        def add_and_store(t, g):
+            y = sb.tile([P, N], F32, name="y%d%d" % (t, g))
+            nc.vector.tensor_tensor(out=y[:], in0=gated[t, g][:], in1=res[t][:, g, :], op=ALU.add)
+            nc.sync.dma_start(out=out[g, m_cols(t), :], in_=y[:])
+
+        multiply(*order[0])
+        for i in range(1, len(order)):
+            multiply(*order[i])
+            add_and_store(*order[i - 1])
+        add_and_store(*order[-1])

@@ -21,7 +21,8 @@ M_TILES = M // M_TILE
 HALF = N // 2
 RUN = 4
 SQUARE = 32
-X_SPLIT = 304
+X_SPLIT = 320
+W_SPLIT = 64
 
 
 def interleave(copy, dst, src):
@@ -53,6 +54,13 @@ def tile_rows_gglu_relu_bias_res_kernel(tc, x, w, u, b, r, out):
         w_raw = sb.tile([P, PACK, M], F32, name="w_raw")
         u_raw = sb.tile([P, PACK, M], F32, name="u_raw")
         nc.sync.dma_start(out=x_raw[:], in_=features(x))
+        b_rows = sb.tile([P, P], F32, name="b_rows", align_bytes=64)
+        b_cols = sb.tile([P, P], F32, name="b_cols", align_bytes=64)
+        nc.vector.memset(b_rows[:], 0.0)
+        nc.sync.dma_start(
+            out=b_rows[0:P:SQUARE, :].rearrange("q (c i) -> q c i", i=SQUARE),
+            in_=b.rearrange("g (t q i) o -> q (g t) (i o)", t=M_TILES, i=SQUARE),
+        )
         nc.sync.dma_start(out=w_raw[:], in_=features(w))
         nc.sync.dma_start(out=u_raw[:], in_=features(u))
         res = []
@@ -64,14 +72,6 @@ def tile_rows_gglu_relu_bias_res_kernel(tc, x, w, u, b, r, out):
             )
             res.append(res_t)
 
-        b_rows = sb.tile([P, P], F32, name="b_rows", align_bytes=64)
-        b_cols = sb.tile([P, P], F32, name="b_cols", align_bytes=64)
-        nc.vector.memset(b_rows[:], 0.0)
-        nc.scalar.dma_start(
-            out=b_rows[0:P:SQUARE, :].rearrange("q (c i) -> q c i", i=SQUARE),
-            in_=b.rearrange("g (t q i) o -> q (g t) (i o)", t=M_TILES, i=SQUARE),
-        )
-        nc.vector.transpose(out=b_cols[:], in_=b_rows[:])
 
         x_lo = sb.tile([P, HALF, PACK], BF16, name="x_lo", align_bytes=64)
         x_hi = sb.tile([P, HALF, PACK], BF16, name="x_hi", align_bytes=64)
@@ -103,8 +103,10 @@ def tile_rows_gglu_relu_bias_res_kernel(tc, x, w, u, b, r, out):
         quantize(nc, x_codes[:, 0:HALF], x_scales[:, 0:HALF], x_lo[:])
         quantize(nc, x_codes[:, HALF:N], x_scales[:, HALF:N], x_hi[:])
 
-        interleave(nc.scalar.copy, w_tiles[0][0][:], w_raw[:, :, m_cols(0)])
-        interleave(nc.vector.tensor_copy, w_tiles[1][0][:], w_raw[:, :, m_cols(1)])
+        interleave(nc.scalar.copy, w_tiles[0][0][:, 0:W_SPLIT, :], w_raw[:, :, 0:W_SPLIT])
+        interleave(nc.vector.tensor_copy, w_tiles[0][0][:, W_SPLIT:M_TILE, :], w_raw[:, :, W_SPLIT:M_TILE])
+        interleave(nc.scalar.copy, w_tiles[1][0][:], w_raw[:, :, m_cols(1)])
+        nc.vector.transpose(out=b_cols[:], in_=b_rows[:])
         quantize_weights(w_tiles[0])
         interleave(nc.vector.tensor_copy, u_tiles[0][0][:], u_raw[:, :, m_cols(0)])
         interleave(nc.scalar.copy, u_tiles[1][0][:], u_raw[:, :, m_cols(1)])
@@ -127,38 +129,59 @@ def tile_rows_gglu_relu_bias_res_kernel(tc, x, w, u, b, r, out):
             )
             return acc
 
-        order = [(t, g) for t in range(M_TILES) for g in range(G)]
         h = {}
         gate = {}
-        for t in range(M_TILES):
-            for g in range(G):
-                h[t, g] = product("h%d%d" % (t, g), w_tiles[t], g)
-            for g in range(G):
-                gate[t, g] = product("gate%d%d" % (t, g), u_tiles[t], g)
+        for g in range(G):
+            h[0, g] = product("h0%d" % g, w_tiles[0], g)
+        for g in range(G):
+            gate[0, g] = product("gate0%d" % g, u_tiles[0], g)
+        for g in range(G):
+            h[1, g] = product("h1%d" % g, w_tiles[1], g)
+            gate[1, g] = product("gate1%d" % g, u_tiles[1], g)
 
         act = {}
-        for t, g in order:
-            col = SQUARE * (g * M_TILES + t)
-            act_tg = sb.tile([P, N], F32, name="act%d%d" % (t, g))
-            nc.scalar.activation(
-                out=act_tg[:], in_=h[t, g][:], func=ACT.Relu, bias=b_cols[:, col : col + 1]
-            )
-            act[t, g] = act_tg
-
         gated = {}
+        y = {}
+        for t in range(M_TILES):
+            for g in range(G):
+                col = SQUARE * (g * M_TILES + t)
+                act[t, g] = sb.tile([P, N], F32, name="act%d%d" % (t, g))
+                gated[t, g] = sb.tile([P, N], F32, name="gated%d%d" % (t, g))
+                y[t, g] = sb.tile([P, N], F32, name="y%d%d" % (t, g))
+                nc.scalar.activation(
+                    out=act[t, g][:], in_=h[t, g][:], func=ACT.Relu, bias=b_cols[:, col : col + 1]
+                )
 
-        def multiply(t, g):
-            gated_tg = sb.tile([P, N], F32, name="gated%d%d" % (t, g))
-            nc.vector.tensor_tensor(out=gated_tg[:], in0=gate[t, g][:], in1=act[t, g][:], op=ALU.mult)
-            gated[t, g] = gated_tg
+        left, right, whole = slice(0, HALF), slice(HALF, N), slice(0, N)
 
-        def add_and_store(t, g):
-            y = sb.tile([P, N], F32, name="y%d%d" % (t, g))
-            nc.vector.tensor_tensor(out=y[:], in0=gated[t, g][:], in1=res[t][:, g, :], op=ALU.add)
-            nc.sync.dma_start(out=out[g, m_cols(t), :], in_=y[:])
+        def multiply(t, g, cols):
+            nc.vector.tensor_tensor(
+                out=gated[t, g][:, cols], in0=gate[t, g][:, cols], in1=act[t, g][:, cols], op=ALU.mult
+            )
 
-        multiply(*order[0])
-        for i in range(1, len(order)):
-            multiply(*order[i])
-            add_and_store(*order[i - 1])
-        add_and_store(*order[-1])
+        def add(engine, t, g, cols):
+            engine.tensor_tensor(
+                out=y[t, g][:, cols], in0=gated[t, g][:, cols], in1=res[t][:, g, cols], op=ALU.add
+            )
+
+        def store(t, g, cols):
+            nc.sync.dma_start(out=out[g, m_cols(t), cols], in_=y[t, g][:, cols])
+
+        multiply(0, 0, left)
+        add(nc.gpsimd, 0, 0, left)
+        multiply(0, 0, right)
+        add(nc.gpsimd, 0, 0, right)
+        store(0, 0, whole)
+        multiply(0, 1, whole)
+        multiply(1, 0, whole)
+        add(nc.vector, 0, 1, whole)
+        store(0, 1, whole)
+        add(nc.gpsimd, 1, 0, left)
+        store(1, 0, left)
+        multiply(1, 1, whole)
+        add(nc.vector, 1, 0, right)
+        store(1, 0, right)
+        add(nc.vector, 1, 1, left)
+        store(1, 1, left)
+        add(nc.vector, 1, 1, right)
+        store(1, 1, right)

from contextlib import ExitStack

import concourse.mybir as mybir

G, D, M, N = 2, 256, 256, 512
FLOPS = 2 * 2 * G * D * M * N

F32 = mybir.dt.float32
BF16 = mybir.dt.bfloat16
U32 = mybir.dt.uint32
U8 = mybir.dt.uint8
FP8X4 = mybir.dt.float8_e4m3fn_x4
ALU = mybir.AluOpType
ACT = mybir.ActivationFunctionType

P = 128
PACK = 4
ROWS = D // PACK
M_TILE = 128
M_TILES = M // M_TILE
HALF = N // 2
RUN = 4
SQUARE = 32
X_SPLIT = 320
W_SPLIT = 64


def interleave(copy, dst, src):
    copy(
        out=dst.rearrange("p (c i) j -> p c j i", i=RUN),
        in_=src.rearrange("p j (c i) -> p c j i", i=RUN),
    )


def quantize(nc, codes, scales, grouped):
    nc.vector.quantize_mx(
        out=codes.bitcast(FP8X4),
        scales=scales,
        in_=grouped.rearrange("p c j -> p (c j)"),
    )


def tile_rows_gglu_relu_bias_res_kernel(tc, x, w, u, b, r, out):
    nc = tc.nc
    with ExitStack() as ctx:
        sb = ctx.enter_context(tc.tile_pool(name="sb", bufs=1))
        psum = ctx.enter_context(tc.psum_pool(name="psum", bufs=1))
        ctx.enter_context(tc.manual_schedule())

        def features(t):
            return t.rearrange("g (p j) c -> (g p) j c", j=PACK)

        x_raw = sb.tile([P, PACK, N], F32, name="x_raw")
        w_raw = sb.tile([P, PACK, M], F32, name="w_raw")
        u_raw = sb.tile([P, PACK, M], F32, name="u_raw")
        nc.sync.dma_start(out=x_raw[:], in_=features(x))
        b_rows = sb.tile([P, P], F32, name="b_rows", align_bytes=64)
        b_cols = sb.tile([P, P], F32, name="b_cols", align_bytes=64)
        nc.vector.memset(b_rows[:], 0.0)
        nc.sync.dma_start(
            out=b_rows[0:P:SQUARE, :].rearrange("q (c i) -> q c i", i=SQUARE),
            in_=b.rearrange("g (t q i) o -> q (g t) (i o)", t=M_TILES, i=SQUARE),
        )
        nc.sync.dma_start(out=w_raw[:], in_=features(w))
        nc.sync.dma_start(out=u_raw[:], in_=features(u))
        res = []
        for t in range(M_TILES):
            res_t = sb.tile([P, G, N], F32, name="res%d" % t)
            nc.sync.dma_start(
                out=res_t[:],
                in_=r[:, t * M_TILE : (t + 1) * M_TILE, :].rearrange("g p n -> p g n"),
            )
            res.append(res_t)


        x_lo = sb.tile([P, HALF, PACK], BF16, name="x_lo", align_bytes=64)
        x_hi = sb.tile([P, HALF, PACK], BF16, name="x_hi", align_bytes=64)
        x_codes = sb.tile([P, N], U32, name="x_codes", align_bytes=64)
        x_scales = sb.tile([P, N], U8, name="x_scales", align_bytes=64)

        def weight_tiles(name):
            tiles = []
            for t in range(M_TILES):
                grouped = sb.tile([P, M_TILE, PACK], BF16, name="%s_bf%d" % (name, t), align_bytes=64)
                codes = sb.tile([P, M_TILE], U32, name="%s_codes%d" % (name, t), align_bytes=64)
                scales = sb.tile([P, M_TILE], U8, name="%s_scales%d" % (name, t), align_bytes=64)
                tiles.append((grouped, codes, scales))
            return tiles

        w_tiles = weight_tiles("w")
        u_tiles = weight_tiles("u")

        def m_cols(t):
            return slice(t * M_TILE, (t + 1) * M_TILE)

        def quantize_weights(tiles):
            grouped, codes, scales = tiles
            quantize(nc, codes[:], scales[:], grouped[:])

        interleave(nc.vector.tensor_copy, x_lo[:], x_raw[:, :, 0:HALF])
        interleave(nc.vector.tensor_copy, x_hi[:, 0 : X_SPLIT - HALF, :], x_raw[:, :, HALF:X_SPLIT])
        interleave(nc.scalar.copy, x_hi[:, X_SPLIT - HALF : HALF, :], x_raw[:, :, X_SPLIT:N])
        quantize(nc, x_codes[:, 0:HALF], x_scales[:, 0:HALF], x_lo[:])
        quantize(nc, x_codes[:, HALF:N], x_scales[:, HALF:N], x_hi[:])

        interleave(nc.scalar.copy, w_tiles[0][0][:, 0:W_SPLIT, :], w_raw[:, :, 0:W_SPLIT])
        interleave(nc.vector.tensor_copy, w_tiles[0][0][:, W_SPLIT:M_TILE, :], w_raw[:, :, W_SPLIT:M_TILE])
        interleave(nc.scalar.copy, w_tiles[1][0][:], w_raw[:, :, m_cols(1)])
        nc.vector.transpose(out=b_cols[:], in_=b_rows[:])
        quantize_weights(w_tiles[0])
        interleave(nc.vector.tensor_copy, u_tiles[0][0][:], u_raw[:, :, m_cols(0)])
        interleave(nc.scalar.copy, u_tiles[1][0][:], u_raw[:, :, m_cols(1)])
        quantize_weights(w_tiles[1])
        quantize_weights(u_tiles[0])
        quantize_weights(u_tiles[1])

        def product(name, tiles, g):
            grouped, codes, scales = tiles
            rows = slice(g * ROWS, (g + 1) * ROWS)
            acc = psum.tile([M_TILE, N], F32, name=name)
            nc.tensor.matmul_mx(
                out=acc[:],
                lhsT=codes[rows, :].bitcast(FP8X4),
                lhsT_scale=scales[rows, :],
                rhs=x_codes[rows, :].bitcast(FP8X4),
                rhs_scale=x_scales[rows, :],
                start=True,
                stop=True,
            )
            return acc

        h = {}
        gate = {}
        for g in range(G):
            h[0, g] = product("h0%d" % g, w_tiles[0], g)
        for g in range(G):
            gate[0, g] = product("gate0%d" % g, u_tiles[0], g)
        for g in range(G):
            h[1, g] = product("h1%d" % g, w_tiles[1], g)
            gate[1, g] = product("gate1%d" % g, u_tiles[1], g)

        act = {}
        gated = {}
        y = {}
        for t in range(M_TILES):
            for g in range(G):
                col = SQUARE * (g * M_TILES + t)
                act[t, g] = sb.tile([P, N], F32, name="act%d%d" % (t, g))
                gated[t, g] = sb.tile([P, N], F32, name="gated%d%d" % (t, g))
                y[t, g] = sb.tile([P, N], F32, name="y%d%d" % (t, g))
                nc.scalar.activation(
                    out=act[t, g][:], in_=h[t, g][:], func=ACT.Relu, bias=b_cols[:, col : col + 1]
                )

        left, right, whole = slice(0, HALF), slice(HALF, N), slice(0, N)

        def multiply(t, g, cols):
            nc.vector.tensor_tensor(
                out=gated[t, g][:, cols], in0=gate[t, g][:, cols], in1=act[t, g][:, cols], op=ALU.mult
            )

        def add(engine, t, g, cols):
            engine.tensor_tensor(
                out=y[t, g][:, cols], in0=gated[t, g][:, cols], in1=res[t][:, g, cols], op=ALU.add
            )

        def store(t, g, cols):
            nc.sync.dma_start(out=out[g, m_cols(t), cols], in_=y[t, g][:, cols])

        multiply(0, 0, left)
        add(nc.gpsimd, 0, 0, left)
        multiply(0, 0, right)
        add(nc.gpsimd, 0, 0, right)
        store(0, 0, whole)
        multiply(0, 1, whole)
        multiply(1, 0, whole)
        add(nc.vector, 0, 1, whole)
        store(0, 1, whole)
        add(nc.gpsimd, 1, 0, left)
        store(1, 0, left)
        multiply(1, 1, whole)
        add(nc.vector, 1, 0, right)
        store(1, 0, right)
        add(nc.vector, 1, 1, left)
        store(1, 1, left)
        add(nc.vector, 1, 1, right)
        store(1, 1, right)
